import numpy as np, ml_dtypes
CORES = [97,101,225,229,353,357,481,485]
N = 8
KB, QP = 4, 128
ROOT = 3
def setup_inputs(rng):
    q = rng.standard_normal((N, 128, QP), dtype=np.float32) / 4; k = rng.standard_normal((N, 128, KB * 128), dtype=np.float32)
    a = 2 * np.pi * rng.random((N, QP)); s = 400 * rng.random((N, QP)) ** 1.5; q[:, 0, :] = s * np.cos(a); q[:, 1, :] = s * np.sin(a); q[:, 2, :] = 150 * rng.standard_normal((N, QP)); k[:, 2, :] = 1 + k[:, 2, :] / 50
    a = (2 * np.pi * rng.random() + np.pi / 2 * (rng.permutation(N).reshape(N, 1, 1) + 0.5) / N - 0.5 + (np.arange(KB).reshape(1, KB, 1) + rng.random((N, KB, 128))) / KB).reshape(N, KB * 128); k[:, 0, :] = np.cos(a); k[:, 1, :] = np.sin(a)
    for t in range(0, QP, 2):
        j, i = (t // 2) % N, rng.integers(KB * 128); q[ROOT, :2, t] = s[ROOT, t] * k[j, :2, i]; q[ROOT, 3:, t] += k[j, 3:, i] / 8
    return {"q": q.astype(ml_dtypes.bfloat16), "k": k.astype(ml_dtypes.bfloat16), "v": rng.standard_normal((N, 128, KB * 128), dtype=np.float32).astype(ml_dtypes.bfloat16)}
def setup_inputs_big(rng):
    d = setup_inputs(rng)
    for k in ("v",): d[k] = (d[k].astype(np.float32) * 1048576.0).astype(d[k].dtype)
    return d
def setup_inputs_small(rng):
    d = setup_inputs(rng)
    for k in ("v",): d[k] = (d[k].astype(np.float32) * (1 / 1048576.0)).astype(d[k].dtype)
    return d
def reference(q, k, v):
    Q, K, V = q.astype(np.float64), k.astype(np.float64), v.astype(np.float64)
    y = np.full((N, QP, 128), np.nan)
    for r in [ROOT]:
        js = list(range(N))
        S = np.concatenate([K[j].T @ Q[r] for j in js], axis=0)
        P = np.exp(S - S.max(axis=0)); P = P / P.sum(axis=0)
        y[r] = P.T @ np.concatenate([V[j][:, 128 * b:128 * b + 128] for j in js for b in range(KB)], axis=0)
    return {"y": y.astype(ml_dtypes.bfloat16)}

@@ -1,0 +1,250 @@
+from concourse.bass import DstId, RemoteDMATransfer
+from concourse.mybir import AluOpType, AxisListType, ActivationFunctionType
+
+B = 128
+KB = 4
+NS = 8
+VW = 136
+OW = B + 1
+MW = 8
+
+SCRATCH = {
+    "qs": ("sbuf", [B, B], "bfloat16"),
+    "ks": ("sbuf", [B, KB * B], "bfloat16"),
+    "vs": ("sbuf", [B, KB * VW], "bfloat16"),
+    "one": ("sbuf", [B, B], "bfloat16"),
+    "idn": ("sbuf", [B, B], "bfloat16"),
+    "pmx": ("sbuf", [B, KB], "float32"),
+    "ngm": ("sbuf", [B, MW], "bfloat16"),
+    "dgm": ("sbuf", [B, B], "bfloat16"),
+    "pt": ("sbuf", [B, KB * B], "bfloat16"),
+    "msg": ("sbuf", [B, VW], "bfloat16"),
+    "mall": ("sbuf", [B, NS * MW], "bfloat16"),
+    "oland": ("sbuf", [B, NS * VW], "bfloat16"),
+    "mng": ("sbuf", [B, 1], "float32"),
+    "wv": ("sbuf", [B, NS], "float32"),
+    "dg": ("sbuf", [B, NS * B], "bfloat16"),
+    "rcp": ("sbuf", [B, 1], "float32"),
+    "ysb": ("sbuf", [B, B], "bfloat16"),
+    "sp0": ("psum", [B, 512], "float32"),
+    "sp1": ("psum", [B, 512], "float32"),
+    "sp2": ("psum", [B, 512], "float32"),
+    "sp3": ("psum", [B, 512], "float32"),
+    "op": ("psum", [B, 512], "float32"),
+    "yp": ("psum", [B, 512], "float32"),
+}
+SEMAPHORES = (["qready", "kready", "vready", "c1", "c2", "idr", "nm", "dgs", "od", "ms", "lsent",
+               "marr", "mn", "wd", "yd", "rc", "ys", "yst"]
+              + ["%s%d" % (n, b) for n in ("st", "rd", "sh", "ex") for b in range(KB)]
+              + ["%s%d" % (n, j) for n in ("dj", "oa") for j in range(NS)])
+
+
+def _bits(mask):
+    return bin(mask).count("1")
+
+
+def _same_chip(topo, a, b):
+    return topo.host(a) == topo.host(b) and topo.chip(a) == topo.chip(b)
+
+
+def _plan(T, topo):
+    cores = [int(c) for c in T.cores]
+    root = cores[T.root]
+    world = range((max(topo.host(c) for c in cores) + 1) * topo.CORES_PER_HOST)
+    site = {}
+    for r, c in enumerate(cores):
+        if c == root or (topo.may_write(root, c) and topo.may_write(c, root)):
+            site[r] = c
+    taken = set(cores)
+    for r, c in enumerate(cores):
+        if r in site:
+            continue
+        cand = [h for h in world
+                if h not in taken and topo.same_plane(c, h) and topo.may_write(c, h)
+                and topo.chip(h) == topo.chip(root) and topo.die(h) == topo.die(c)
+                and topo.may_write(root, h) and topo.may_write(h, root)]
+        site[r] = max(cand)
+        taken.add(site[r])
+    return cores, root, site
+
+
+def _q_order(cores, root, site, topo):
+    near = [r for r in site if site[r] != root and _same_chip(topo, site[r], root)]
+    away = [r for r in site if site[r] != root and r not in near]
+    home = [r for r in away if site[r] == cores[r]]
+    hosts = sorted(set(topo.host(site[r]) for r in home), reverse=True)
+    rows = [[r for r in home if topo.host(site[r]) == h] for h in hosts]
+    order = []
+    for i in range(max(len(x) for x in rows)):
+        order += [x[i] for x in rows if i < len(x)]
+    return order + [r for r in away if r not in home], near
+
+
+def _load_kv(g, T):
+    S = T.sem
+    g.sync.dma_start(T.ks[:], T.k[:, :]).then_inc(S.kready, 16)
+    for b in range(KB):
+        g.sync.dma_start(T.vs[:, VW * b:VW * b + B], T.v[:, B * b:B * b + B]).then_inc(S.vready, 16)
+    for b in range(KB):
+        g.vector.memset(T.vs[:, VW * b + B:VW * (b + 1)], 1.0).then_inc(S.c2, 1)
+
+
+def _ship(g, core, dst, T, topo):
+    S = T.sem
+    _load_kv(g, T)
+    rid, pid = topo.addr(dst, core)
+    mask = topo.mask(core, dst)
+    g.wait_ge(S.kready, 16)
+    g.remote_dma(out_ap=T.ks[:], in_ap=T.ks[:], remote_sem=S.kready, local_sem=S.lsent,
+                 pid=pid, routing_id=rid, dma_engine_mask=mask)
+    g.wait_ge(S.vready, 16 * KB)
+    g.wait_ge(S.c2, KB)
+    g.remote_dma(out_ap=T.vs[:], in_ap=T.vs[:], remote_sem=S.vready, local_sem=S.lsent,
+                 pid=pid, routing_id=rid, dma_engine_mask=mask)
+    g.wait_ge(S.lsent, 2 * _bits(mask))
+
+
+def _consts(g, T):
+    S = T.sem
+    g.vector.memset(T.one[:], 1.0).then_inc(S.c1, 1)
+    g.wait_ge(S.c1, 1)
+    g.affine_select(T.idn[:], T.one[:], [[-1, B]], AluOpType.is_equal, 0.0, 0, 1).then_inc(S.idr, 1)
+
+
+def _site(g, T, nq, nk, nv, n_ones, negm, msg):
+    S = T.sem
+    pe, dve, act = g.tensor, g.vector, g.scalar
+    sp = [T["sp%d" % b] for b in range(KB)]
+    kb = [T.ks[:, B * b:B * (b + 1)] for b in range(KB)]
+
+    pe.wait_ge(S.qready, nq)
+    pe.wait_ge(S.kready, nk)
+    for b in range(KB):
+        pe.matmul(sp[b][:, 0:B], T.qs[:], kb[b], True, True).then_inc(S["st%d" % b], 1)
+    for b in range(KB):
+        dve.wait_ge(S["st%d" % b], 1)
+        dve.tensor_reduce(T.pmx[:, b:b + 1], sp[b][:, 0:B], AxisListType.X, AluOpType.max).then_inc(S["rd%d" % b], 1)
+    for b in range(KB):
+        dve.wait_ge(S["rd%d" % b], 1)
+    dve.tensor_reduce(negm, T.pmx[:, 0:KB], AxisListType.X, AluOpType.max, negate=True).then_inc(S.nm, 1)
+    dve.wait_ge(S.nm, 1)
+    dve.wait_ge(S.idr, 1)
+    dve.tensor_scalar(T.dgm[:], T.idn[:], negm, None, AluOpType.mult).then_inc(S.dgs, 1)
+
+    def open_block(b):
+        pe.wait_ge(S["rd%d" % b], 1)
+        pe.matmul(sp[b][:, B:2 * B], kb[b], T.qs[:], True, False)
+
+    def shift_block(b):
+        pe.matmul(sp[b][:, B:2 * B], T.one[:], T.dgm[:], False, True).then_inc(S["sh%d" % b], 1)
+
+    open_block(0)
+    open_block(1)
+    pe.wait_ge(S.c1, 1)
+    pe.wait_ge(S.dgs, 1)
+    shift_block(0)
+    shift_block(1)
+    for b in range(2, KB):
+        open_block(b)
+        shift_block(b)
+    for b in range(KB):
+        act.wait_ge(S["sh%d" % b], 1)
+        act.activation(T.pt[:, B * b:B * (b + 1)], sp[b][:, B:2 * B],
+                       ActivationFunctionType.Exp).then_inc(S["ex%d" % b], 1)
+    pe.wait_ge(S.vready, nv)
+    if n_ones:
+        pe.wait_ge(S.c2, n_ones)
+    for b in range(KB):
+        pe.wait_ge(S["ex%d" % b], 1)
+        mm = pe.matmul(T.op[:, 0:OW], T.pt[:, B * b:B * (b + 1)], T.vs[:, VW * b:VW * b + OW], b == 0, b == KB - 1)
+    mm.then_inc(S.od, 1)
+    dve.wait_ge(S.od, 1)
+    dve.tensor_copy(msg, T.op[:, 0:OW]).then_inc(S.ms, 1)
+
+
+def rank_program(g, core, T, topo):
+    cores, root, site = _plan(T, topo)
+    rank = T.rank_of(core)
+    if rank is not None and site[rank] != core:
+        _ship(g, core, site[rank], T, topo)
+        return
+    mine = [r for r in site if site[r] == core]
+    if not mine:
+        return
+    slot = mine[0]
+    S = T.sem
+    away, near = _q_order(cores, root, site, topo)
+    away_mask = topo.mask(root, site[away[0]])
+    for r in away:
+        away_mask &= topo.mask(root, site[r])
+    near_mask = {r: (topo.mask(root, site[r]) & ~away_mask) for r in near}
+
+    if core != root:
+        _consts(g, T)
+        if rank is not None:
+            _load_kv(g, T)
+            nk, nv, n_ones = 16, 16 * KB, KB
+        else:
+            n = _bits(topo.mask(cores[slot], core))
+            nk, nv, n_ones = n, n, 0
+        nq = _bits(near_mask[slot]) if slot in near else _bits(away_mask)
+        _site(g, T, nq, nk, nv, n_ones, T.ngm[:, 0:1], T.msg[:, 0:OW])
+        rid, pid = topo.addr(root, core)
+        mask = topo.mask(core, root)
+        g.wait_ge(S.nm, 1)
+        g.remote_dma(out_ap=T.mall[:, MW * slot:MW * slot + 1], in_ap=T.ngm[:, 0:1], remote_sem=S.marr,
+                     local_sem=S.lsent, pid=pid, routing_id=rid, dma_engine_mask=mask)
+        g.wait_ge(S.ms, 1)
+        g.remote_dma(out_ap=T.oland[:, VW * slot:VW * slot + OW], in_ap=T.msg[:, 0:OW], remote_sem=S["oa%d" % slot],
+                     local_sem=S.lsent, pid=pid, routing_id=rid, dma_engine_mask=mask)
+        g.wait_ge(S.lsent, 2 * _bits(mask))
+        return
+
+    pe, dve, act = g.tensor, g.vector, g.scalar
+    g.sync.dma_start(T.qs[:], T.q[:, :]).then_inc(S.qready, 16)
+    _consts(g, T)
+    _load_kv(g, T)
+    g.wait_ge(S.qready, 16)
+    ids = [topo.addr(site[r], root) for r in away]
+    g.remote_dma_fused([RemoteDMATransfer(dst_ids=[DstId(rid=a, pnc=p) for a, p in ids], dma_engine_mask=away_mask,
+                                          remote_sem=S.qready, srcs=[T.qs[:]], dsts=[T.qs[:] for _ in ids], alu_op=0)],
+                       local_sem=S.lsent)
+    left = _bits(away_mask)
+    for r in near:
+        rid, pid = topo.addr(site[r], root)
+        g.remote_dma(out_ap=T.qs[:], in_ap=T.qs[:], remote_sem=S.qready, local_sem=S.lsent,
+                     pid=pid, routing_id=rid, dma_engine_mask=near_mask[r])
+        left += _bits(near_mask[r])
+    g.wait_ge(S.lsent, left)
+
+    _site(g, T, 16, 16, 16 * KB, KB, T.mall[:, MW * slot:MW * slot + 1], T.oland[:, VW * slot:VW * slot + OW])
+
+    n_m = sum(_bits(topo.mask(site[r], root)) for r in site if r != slot)
+    shifts = T.mall[:, 0:NS * MW:MW]
+    dve.wait_ge(S.marr, n_m)
+    dve.tensor_reduce(T.mng[:, 0:1], shifts, AxisListType.X, AluOpType.min).then_inc(S.mn, 1)
+    act.wait_ge(S.marr, n_m)
+    act.wait_ge(S.nm, 1)
+    act.wait_ge(S.mn, 1)
+    act.activation(T.wv[:, 0:NS], shifts, ActivationFunctionType.Exp, bias=T.mng[:, 0:1], scale=-1.0).then_inc(S.wd, 1)
+    order = [slot] + near + away
+    dve.wait_ge(S.wd, 1)
+    for j in order:
+        dve.tensor_scalar(T.dg[:, B * j:B * (j + 1)], T.idn[:], T.wv[:, j:j + 1], None,
+                          AluOpType.mult).then_inc(S["dj%d" % j], 1)
+    for i, j in enumerate(order):
+        pe.wait_ge(S["dj%d" % j], 1)
+        if j == slot:
+            pe.wait_ge(S.ms, 1)
+        else:
+            pe.wait_ge(S["oa%d" % j], _bits(topo.mask(site[j], root)))
+        mm = pe.matmul(T.yp[:, 0:OW], T.dg[:, B * j:B * (j + 1)], T.oland[:, VW * j:VW * j + OW],
+                       i == 0, i == len(order) - 1)
+    mm.then_inc(S.yd, 1)
+    dve.wait_ge(S.yd, 1)
+    dve.reciprocal(T.rcp[:, 0:1], T.yp[:, B:OW]).then_inc(S.rc, 1)
+    dve.wait_ge(S.rc, 1)
+    dve.tensor_scalar(T.ysb[:], T.yp[:, 0:B], T.rcp[:, 0:1], None, AluOpType.mult).then_inc(S.ys, 1)
+    g.sync.wait_ge(S.ys, 1)
+    g.sync.dma_start(T.y[:, :], T.ysb[:]).then_inc(S.yst, 16)
+    g.sync.wait_ge(S.yst, 16)

@@ -33,7 +33,7 @@ SCRATCH = {
     "op": ("psum", [B, 512], "float32"),
     "yp": ("psum", [B, 512], "float32"),
 }
-SEMAPHORES = (["qready", "kready", "vready", "c1", "c2", "idr", "nm", "dgs", "od", "ms", "lsent",
+SEMAPHORES = (["qready", "kready", "vready", "c0", "c1", "c2", "idr", "nm", "dgs", "od", "ms", "lsent",
                "marr", "mn", "wd", "yd", "rc", "ys", "yst"]
               + ["%s%d" % (n, b) for n in ("st", "rd", "sh", "ex") for b in range(KB)]
               + ["%s%d" % (n, j) for n in ("dj", "oa") for j in range(NS)])
@@ -104,9 +104,15 @@ def _ship(g, core, dst, T, topo):
     g.wait_ge(S.lsent, 2 * _bits(mask))
 
 
-def _consts(g, T):
+def _ones(g, T):
     S = T.sem
-    g.vector.memset(T.one[:], 1.0).then_inc(S.c1, 1)
+    g.vector.memset(T.one[:], 0.0).then_inc(S.c0, 1)
+    g.scalar.wait_ge(S.c0, 1)
+    g.scalar.activation(T.one[:], T.one[:], ActivationFunctionType.Exp).then_inc(S.c1, 1)
+
+
+def _identity(g, T):
+    S = T.sem
     g.wait_ge(S.c1, 1)
     g.affine_select(T.idn[:], T.one[:], [[-1, B]], AluOpType.is_equal, 0.0, 0, 1).then_inc(S.idr, 1)
 
@@ -131,22 +137,13 @@ def _site(g, T, nq, nk, nv, n_ones, negm, msg):
     dve.wait_ge(S.idr, 1)
     dve.tensor_scalar(T.dgm[:], T.idn[:], negm, None, AluOpType.mult).then_inc(S.dgs, 1)
 
-    def open_block(b):
+    for b in range(KB):
         pe.wait_ge(S["rd%d" % b], 1)
         pe.matmul(sp[b][:, B:2 * B], kb[b], T.qs[:], True, False)
-
-    def shift_block(b):
-        pe.matmul(sp[b][:, B:2 * B], T.one[:], T.dgm[:], False, True).then_inc(S["sh%d" % b], 1)
-
-    open_block(0)
-    open_block(1)
     pe.wait_ge(S.c1, 1)
     pe.wait_ge(S.dgs, 1)
-    shift_block(0)
-    shift_block(1)
-    for b in range(2, KB):
-        open_block(b)
-        shift_block(b)
+    for b in range(KB):
+        pe.matmul(sp[b][:, B:2 * B], T.one[:], T.dgm[:], False, True).then_inc(S["sh%d" % b], 1)
     for b in range(KB):
         act.wait_ge(S["sh%d" % b], 1)
         act.activation(T.pt[:, B * b:B * (b + 1)], sp[b][:, B:2 * B],
@@ -180,7 +177,8 @@ def rank_program(g, core, T, topo):
     near_mask = {r: (topo.mask(root, site[r]) & ~away_mask) for r in near}
 
     if core != root:
-        _consts(g, T)
+        _ones(g, T)
+        _identity(g, T)
         if rank is not None:
             _load_kv(g, T)
             nk, nv, n_ones = 16, 16 * KB, KB
@@ -202,7 +200,7 @@ def rank_program(g, core, T, topo):
 
     pe, dve, act = g.tensor, g.vector, g.scalar
     g.sync.dma_start(T.qs[:], T.q[:, :]).then_inc(S.qready, 16)
-    _consts(g, T)
+    _ones(g, T)
     _load_kv(g, T)
     g.wait_ge(S.qready, 16)
     ids = [topo.addr(site[r], root) for r in away]
@@ -215,6 +213,7 @@ def rank_program(g, core, T, topo):
         g.remote_dma(out_ap=T.qs[:], in_ap=T.qs[:], remote_sem=S.qready, local_sem=S.lsent,
                      pid=pid, routing_id=rid, dma_engine_mask=near_mask[r])
         left += _bits(near_mask[r])
+    _identity(g, T)
     g.wait_ge(S.lsent, left)
 
     _site(g, T, 16, 16, 16 * KB, KB, T.mall[:, MW * slot:MW * slot + 1], T.oland[:, VW * slot:VW * slot + OW])

@@ -4,6 +4,8 @@ from concourse.mybir import AluOpType, AxisListType, ActivationFunctionType
 B = 128
 KB = 4
 NS = 8
+NG = 5
+NP = 5
 VW = 136
 OW = B + 1
 MW = 8
@@ -12,12 +14,14 @@ SCRATCH = {
     "qs": ("sbuf", [B, B], "bfloat16"),
     "ks": ("sbuf", [B, KB * B], "bfloat16"),
     "vs": ("sbuf", [B, KB * VW], "bfloat16"),
+    "gks": ("sbuf", [B, NG * B], "bfloat16"),
+    "gvs": ("sbuf", [B, NG * VW], "bfloat16"),
     "one": ("sbuf", [B, B], "bfloat16"),
     "idn": ("sbuf", [B, B], "bfloat16"),
-    "pmx": ("sbuf", [B, KB], "float32"),
+    "pmx": ("sbuf", [B, 2 * 8], "float32"),
     "ngm": ("sbuf", [B, MW], "bfloat16"),
-    "dgm": ("sbuf", [B, B], "bfloat16"),
-    "pt": ("sbuf", [B, KB * B], "bfloat16"),
+    "dgm": ("sbuf", [B, 2 * B], "bfloat16"),
+    "pt": ("sbuf", [B, 2 * NP * B], "bfloat16"),
     "msg": ("sbuf", [B, VW], "bfloat16"),
     "mall": ("sbuf", [B, NS * MW], "bfloat16"),
     "oland": ("sbuf", [B, NS * VW], "bfloat16"),
@@ -30,17 +34,25 @@ SCRATCH = {
     "sp1": ("psum", [B, 512], "float32"),
     "sp2": ("psum", [B, 512], "float32"),
     "sp3": ("psum", [B, 512], "float32"),
+    "sp4": ("psum", [B, 512], "float32"),
     "op": ("psum", [B, 512], "float32"),
     "yp": ("psum", [B, 512], "float32"),
 }
-SEMAPHORES = (["qready", "kready", "vready", "c0", "c1", "c2", "idr", "nm", "dgs", "od", "ms", "lsent",
+SEMAPHORES = (["qready", "kready", "vready", "gk", "gv", "c0", "c1", "c2", "idr", "lsent",
                "marr", "mn", "wd", "yd", "rc", "ys", "yst"]
-              + ["%s%d" % (n, b) for n in ("st", "rd", "sh", "ex") for b in range(KB)]
+              + ["%s%d" % (n, p) for n in ("nm", "dgs", "od", "ms") for p in range(2)]
+              + ["%s%d%d" % (n, p, b) for n in ("st", "rd", "sh", "ex") for p in range(2) for b in range(NP)]
               + ["%s%d" % (n, j) for n in ("dj", "oa") for j in range(NS)])
 
 
 def _bits(mask):
     return bin(mask).count("1")
+
+
+def _split(mask, n):
+    eng = [i for i in range(mask.bit_length()) if (mask >> i) & 1]
+    per = len(eng) // n
+    return [sum(1 << i for i in eng[j * per:(j + 1) * per]) for j in range(n)]
 
 
 def _same_chip(topo, a, b):
@@ -50,34 +62,37 @@ def _same_chip(topo, a, b):
 def _plan(T, topo):
     cores = [int(c) for c in T.cores]
     root = cores[T.root]
-    world = range((max(topo.host(c) for c in cores) + 1) * topo.CORES_PER_HOST)
-    site = {}
-    for r, c in enumerate(cores):
-        if c == root or (topo.may_write(root, c) and topo.may_write(c, root)):
-            site[r] = c
-    taken = set(cores)
-    for r, c in enumerate(cores):
-        if r in site:
-            continue
-        cand = [h for h in world
-                if h not in taken and topo.same_plane(c, h) and topo.may_write(c, h)
-                and topo.chip(h) == topo.chip(root) and topo.die(h) == topo.die(c)
-                and topo.may_write(root, h) and topo.may_write(h, root)]
-        site[r] = max(cand)
-        taken.add(site[r])
-    return cores, root, site
+    sites = [c for c in cores if c == root or (topo.may_write(root, c) and topo.may_write(c, root))]
+    far = [c for c in cores if c not in sites]
+    ship = {c: [] for c in cores}
+    keep = {c: list(range(KB)) for c in sites}
+    guests = {c: 0 for c in sites}
+    for c in far:
+        cand = [s for s in sites if topo.may_write(c, s) and topo.die(s) == topo.die(c)]
+        common = topo.mask(c, cand[0])
+        for s in cand:
+            common &= topo.mask(c, s)
+        parts = _split(common, len(cand))
+        per = KB // len(cand)
+        for i, s in enumerate(cand):
+            ship[c].append((s, per * i, per, guests[s], parts[i]))
+            guests[s] += per
+    for s in sites:
+        if s != root:
+            ship[s].append((root, keep[s].pop(), 1, guests[root], topo.mask(s, root)))
+            guests[root] += 1
+    return cores, root, sites, far, ship, keep, guests
 
 
-def _q_order(cores, root, site, topo):
-    near = [r for r in site if site[r] != root and _same_chip(topo, site[r], root)]
-    away = [r for r in site if site[r] != root and r not in near]
-    home = [r for r in away if site[r] == cores[r]]
-    hosts = sorted(set(topo.host(site[r]) for r in home), reverse=True)
-    rows = [[r for r in home if topo.host(site[r]) == h] for h in hosts]
+def _q_order(root, sites, topo):
+    near = [c for c in sites if c != root and _same_chip(topo, c, root)]
+    away = [c for c in sites if c != root and c not in near]
+    hosts = sorted(set(topo.host(c) for c in away), reverse=True)
+    rows = [[c for c in away if topo.host(c) == h] for h in hosts]
     order = []
     for i in range(max(len(x) for x in rows)):
         order += [x[i] for x in rows if i < len(x)]
-    return order + [r for r in away if r not in home], near
+    return order, near
 
 
 def _load_kv(g, T):
@@ -89,19 +104,22 @@ def _load_kv(g, T):
         g.vector.memset(T.vs[:, VW * b + B:VW * (b + 1)], 1.0).then_inc(S.c2, 1)
 
 
-def _ship(g, core, dst, T, topo):
+def _ship(g, core, T, topo, ships):
     S = T.sem
-    _load_kv(g, T)
-    rid, pid = topo.addr(dst, core)
-    mask = topo.mask(core, dst)
+
+    def call(src, dst, w, sem):
+        g.remote_dma_fused(
+            [RemoteDMATransfer(dst_ids=[DstId(rid=topo.addr(d, core)[0], pnc=topo.addr(d, core)[1])],
+                               dma_engine_mask=m, remote_sem=sem, srcs=[src[:, w * b0:w * (b0 + nb)]],
+                               dsts=[dst[:, w * s0:w * (s0 + nb)]], alu_op=0)
+             for d, b0, nb, s0, m in ships], local_sem=S.lsent)
+
     g.wait_ge(S.kready, 16)
-    g.remote_dma(out_ap=T.ks[:], in_ap=T.ks[:], remote_sem=S.kready, local_sem=S.lsent,
-                 pid=pid, routing_id=rid, dma_engine_mask=mask)
+    call(T.ks, T.gks, B, S.gk)
     g.wait_ge(S.vready, 16 * KB)
     g.wait_ge(S.c2, KB)
-    g.remote_dma(out_ap=T.vs[:], in_ap=T.vs[:], remote_sem=S.vready, local_sem=S.lsent,
-                 pid=pid, routing_id=rid, dma_engine_mask=mask)
-    g.wait_ge(S.lsent, 2 * _bits(mask))
+    call(T.vs, T.gvs, VW, S.gv)
+    return 2 * sum(_bits(x[4]) for x in ships)
 
 
 def _ones(g, T):
@@ -117,85 +135,104 @@ def _identity(g, T):
     g.affine_select(T.idn[:], T.one[:], [[-1, B]], AluOpType.is_equal, 0.0, 0, 1).then_inc(S.idr, 1)
 
 
-def _site(g, T, nq, nk, nv, n_ones, negm, msg):
+def _site(g, T, p, blocks, nq, need, negm, msg, after=None):
     S = T.sem
     pe, dve, act = g.tensor, g.vector, g.scalar
-    sp = [T["sp%d" % b] for b in range(KB)]
-    kb = [T.ks[:, B * b:B * (b + 1)] for b in range(KB)]
+    nb = len(blocks)
+    sp = [T["sp%d" % b] for b in range(nb)]
+    pt = [T.pt[:, B * (NP * p + b):B * (NP * p + b + 1)] for b in range(nb)]
+    dgm = T.dgm[:, B * p:B * (p + 1)]
+
+    def s1(n):
+        return S["%s%d" % (n, p)]
+
+    def s2(n, b):
+        return S["%s%d%d" % (n, p, b)]
+
+    groups = []
+    for b, blk in enumerate(blocks):
+        if not groups or groups[-1][0] != blk[2]:
+            groups.append((blk[2], []))
+        groups[-1][1].append(b)
 
     pe.wait_ge(S.qready, nq)
-    pe.wait_ge(S.kready, nk)
-    for b in range(KB):
-        pe.matmul(sp[b][:, 0:B], T.qs[:], kb[b], True, True).then_inc(S["st%d" % b], 1)
-    for b in range(KB):
-        dve.wait_ge(S["st%d" % b], 1)
-        dve.tensor_reduce(T.pmx[:, b:b + 1], sp[b][:, 0:B], AxisListType.X, AluOpType.max).then_inc(S["rd%d" % b], 1)
-    for b in range(KB):
-        dve.wait_ge(S["rd%d" % b], 1)
-    dve.tensor_reduce(negm, T.pmx[:, 0:KB], AxisListType.X, AluOpType.max, negate=True).then_inc(S.nm, 1)
-    dve.wait_ge(S.nm, 1)
+    for kind, bs in groups:
+        for sem, n in need[kind][0]:
+            pe.wait_ge(sem, n)
+        for b in bs:
+            pe.matmul(sp[b][:, 0:B], T.qs[:], blocks[b][0], True, True).then_inc(s2("st", b), 1)
+        for b in bs:
+            pe.wait_ge(s2("rd", b), 1)
+            pe.matmul(sp[b][:, B:2 * B], blocks[b][0], T.qs[:], True, False)
+    for b in range(nb):
+        dve.wait_ge(s2("st", b), 1)
+        dve.tensor_reduce(T.pmx[:, 8 * p + b:8 * p + b + 1], sp[b][:, 0:B], AxisListType.X,
+                          AluOpType.max).then_inc(s2("rd", b), 1)
+    for b in range(nb):
+        dve.wait_ge(s2("rd", b), 1)
+    dve.tensor_reduce(negm, T.pmx[:, 8 * p:8 * p + nb], AxisListType.X, AluOpType.max, negate=True).then_inc(s1("nm"), 1)
+    dve.wait_ge(s1("nm"), 1)
     dve.wait_ge(S.idr, 1)
-    dve.tensor_scalar(T.dgm[:], T.idn[:], negm, None, AluOpType.mult).then_inc(S.dgs, 1)
+    dve.tensor_scalar(dgm, T.idn[:], negm, None, AluOpType.mult).then_inc(s1("dgs"), 1)
 
-    for b in range(KB):
-        pe.wait_ge(S["rd%d" % b], 1)
-        pe.matmul(sp[b][:, B:2 * B], kb[b], T.qs[:], True, False)
     pe.wait_ge(S.c1, 1)
-    pe.wait_ge(S.dgs, 1)
-    for b in range(KB):
-        pe.matmul(sp[b][:, B:2 * B], T.one[:], T.dgm[:], False, True).then_inc(S["sh%d" % b], 1)
-    for b in range(KB):
-        act.wait_ge(S["sh%d" % b], 1)
-        act.activation(T.pt[:, B * b:B * (b + 1)], sp[b][:, B:2 * B],
-                       ActivationFunctionType.Exp).then_inc(S["ex%d" % b], 1)
-    pe.wait_ge(S.vready, nv)
-    if n_ones:
-        pe.wait_ge(S.c2, n_ones)
-    for b in range(KB):
-        pe.wait_ge(S["ex%d" % b], 1)
-        mm = pe.matmul(T.op[:, 0:OW], T.pt[:, B * b:B * (b + 1)], T.vs[:, VW * b:VW * b + OW], b == 0, b == KB - 1)
-    mm.then_inc(S.od, 1)
-    dve.wait_ge(S.od, 1)
-    dve.tensor_copy(msg, T.op[:, 0:OW]).then_inc(S.ms, 1)
+    pe.wait_ge(s1("dgs"), 1)
+    for b in range(nb):
+        pe.matmul(sp[b][:, B:2 * B], T.one[:], dgm, False, True).then_inc(s2("sh", b), 1)
+    for b in range(nb):
+        act.wait_ge(s2("sh", b), 1)
+        act.activation(pt[b], sp[b][:, B:2 * B], ActivationFunctionType.Exp).then_inc(s2("ex", b), 1)
+    if after is not None:
+        pe.wait_ge(after, 1)
+    for kind, bs in groups:
+        for sem, n in need[kind][1]:
+            pe.wait_ge(sem, n)
+        for b in bs:
+            pe.wait_ge(s2("ex", b), 1)
+            mm = pe.matmul(T.op[:, 0:OW], pt[b], blocks[b][1], b == 0, b == nb - 1)
+    mm.then_inc(s1("od"), 1)
+    dve.wait_ge(s1("od"), 1)
+    dve.tensor_copy(msg, T.op[:, 0:OW]).then_inc(s1("ms"), 1)
 
 
 def rank_program(g, core, T, topo):
-    cores, root, site = _plan(T, topo)
-    rank = T.rank_of(core)
-    if rank is not None and site[rank] != core:
-        _ship(g, core, site[rank], T, topo)
-        return
-    mine = [r for r in site if site[r] == core]
-    if not mine:
-        return
-    slot = mine[0]
+    cores, root, sites, far, ship, keep, guests = _plan(T, topo)
     S = T.sem
-    away, near = _q_order(cores, root, site, topo)
-    away_mask = topo.mask(root, site[away[0]])
-    for r in away:
-        away_mask &= topo.mask(root, site[r])
-    near_mask = {r: (topo.mask(root, site[r]) & ~away_mask) for r in near}
+    if core in far:
+        _load_kv(g, T)
+        g.wait_ge(S.lsent, _ship(g, core, T, topo, ship[core]))
+        return
+    if core not in sites:
+        return
+    slot = sites.index(core)
+    away, near = _q_order(root, sites, topo)
+    away_mask = topo.mask(root, away[0])
+    for c in away:
+        away_mask &= topo.mask(root, c)
+    near_mask = {c: (topo.mask(root, c) & ~away_mask) for c in near}
+
+    landing = sum(_bits(x[4]) for c in cores for x in ship[c] if x[0] == core)
+    need = {"own": ([(S.kready, 16)], [(S.vready, 16 * KB), (S.c2, KB)]),
+            "guest": ([(S.gk, landing)], [(S.gv, landing)])}
+    own = [(T.ks[:, B * b:B * (b + 1)], T.vs[:, VW * b:VW * b + OW], "own") for b in keep[core]]
+    guest = [(T.gks[:, B * s:B * (s + 1)], T.gvs[:, VW * s:VW * s + OW], "guest") for s in range(guests[core])]
 
     if core != root:
         _ones(g, T)
         _identity(g, T)
-        if rank is not None:
-            _load_kv(g, T)
-            nk, nv, n_ones = 16, 16 * KB, KB
-        else:
-            n = _bits(topo.mask(cores[slot], core))
-            nk, nv, n_ones = n, n, 0
-        nq = _bits(near_mask[slot]) if slot in near else _bits(away_mask)
-        _site(g, T, nq, nk, nv, n_ones, T.ngm[:, 0:1], T.msg[:, 0:OW])
+        _load_kv(g, T)
+        left = _ship(g, core, T, topo, ship[core])
+        nq = _bits(near_mask[core]) if core in near else _bits(away_mask)
+        _site(g, T, 0, own + guest, nq, need, T.ngm[:, 0:1], T.msg[:, 0:OW])
         rid, pid = topo.addr(root, core)
         mask = topo.mask(core, root)
-        g.wait_ge(S.nm, 1)
+        g.wait_ge(S.nm0, 1)
         g.remote_dma(out_ap=T.mall[:, MW * slot:MW * slot + 1], in_ap=T.ngm[:, 0:1], remote_sem=S.marr,
                      local_sem=S.lsent, pid=pid, routing_id=rid, dma_engine_mask=mask)
-        g.wait_ge(S.ms, 1)
+        g.wait_ge(S.ms0, 1)
         g.remote_dma(out_ap=T.oland[:, VW * slot:VW * slot + OW], in_ap=T.msg[:, 0:OW], remote_sem=S["oa%d" % slot],
                      local_sem=S.lsent, pid=pid, routing_id=rid, dma_engine_mask=mask)
-        g.wait_ge(S.lsent, 2 * _bits(mask))
+        g.wait_ge(S.lsent, left + 2 * _bits(mask))
         return
 
     pe, dve, act = g.tensor, g.vector, g.scalar
@@ -203,30 +240,35 @@ def rank_program(g, core, T, topo):
     _ones(g, T)
     _load_kv(g, T)
     g.wait_ge(S.qready, 16)
-    ids = [topo.addr(site[r], root) for r in away]
+    ids = [topo.addr(c, root) for c in away]
     g.remote_dma_fused([RemoteDMATransfer(dst_ids=[DstId(rid=a, pnc=p) for a, p in ids], dma_engine_mask=away_mask,
                                           remote_sem=S.qready, srcs=[T.qs[:]], dsts=[T.qs[:] for _ in ids], alu_op=0)],
                        local_sem=S.lsent)
     left = _bits(away_mask)
-    for r in near:
-        rid, pid = topo.addr(site[r], root)
+    for c in near:
+        rid, pid = topo.addr(c, root)
         g.remote_dma(out_ap=T.qs[:], in_ap=T.qs[:], remote_sem=S.qready, local_sem=S.lsent,
-                     pid=pid, routing_id=rid, dma_engine_mask=near_mask[r])
-        left += _bits(near_mask[r])
+                     pid=pid, routing_id=rid, dma_engine_mask=near_mask[c])
+        left += _bits(near_mask[c])
     _identity(g, T)
     g.wait_ge(S.lsent, left)
 
-    _site(g, T, 16, 16, 16 * KB, KB, T.mall[:, MW * slot:MW * slot + 1], T.oland[:, VW * slot:VW * slot + OW])
+    gslot = len(sites)
+    ns = gslot + 1
+    _site(g, T, 0, own, 16, need, T.mall[:, MW * slot:MW * slot + 1], T.oland[:, VW * slot:VW * slot + OW])
+    _site(g, T, 1, guest, 16, need, T.mall[:, MW * gslot:MW * gslot + 1], T.oland[:, VW * gslot:VW * gslot + OW],
+          after=S.ms0)
 
-    n_m = sum(_bits(topo.mask(site[r], root)) for r in site if r != slot)
-    shifts = T.mall[:, 0:NS * MW:MW]
+    n_m = sum(_bits(topo.mask(c, root)) for c in sites if c != root)
+    shifts = T.mall[:, 0:ns * MW:MW]
     dve.wait_ge(S.marr, n_m)
     dve.tensor_reduce(T.mng[:, 0:1], shifts, AxisListType.X, AluOpType.min).then_inc(S.mn, 1)
     act.wait_ge(S.marr, n_m)
-    act.wait_ge(S.nm, 1)
+    act.wait_ge(S.nm0, 1)
+    act.wait_ge(S.nm1, 1)
     act.wait_ge(S.mn, 1)
-    act.activation(T.wv[:, 0:NS], shifts, ActivationFunctionType.Exp, bias=T.mng[:, 0:1], scale=-1.0).then_inc(S.wd, 1)
-    order = [slot] + near + away
+    act.activation(T.wv[:, 0:ns], shifts, ActivationFunctionType.Exp, bias=T.mng[:, 0:1], scale=-1.0).then_inc(S.wd, 1)
+    order = [slot, gslot] + [sites.index(c) for c in near + away]
     dve.wait_ge(S.wd, 1)
     for j in order:
         dve.tensor_scalar(T.dg[:, B * j:B * (j + 1)], T.idn[:], T.wv[:, j:j + 1], None,
@@ -234,9 +276,11 @@ def rank_program(g, core, T, topo):
     for i, j in enumerate(order):
         pe.wait_ge(S["dj%d" % j], 1)
         if j == slot:
-            pe.wait_ge(S.ms, 1)
+            pe.wait_ge(S.ms0, 1)
+        elif j == gslot:
+            pe.wait_ge(S.ms1, 1)
         else:
-            pe.wait_ge(S["oa%d" % j], _bits(topo.mask(site[j], root)))
+            pe.wait_ge(S["oa%d" % j], _bits(topo.mask(sites[j], root)))
         mm = pe.matmul(T.yp[:, 0:OW], T.dg[:, B * j:B * (j + 1)], T.oland[:, VW * j:VW * j + OW],
                        i == 0, i == len(order) - 1)
     mm.then_inc(S.yd, 1)

@@ -13,9 +13,10 @@ MW = 8
 SCRATCH = {
     "qs": ("sbuf", [B, B], "bfloat16"),
     "ks": ("sbuf", [B, KB * B], "bfloat16"),
-    "vs": ("sbuf", [B, KB * VW], "bfloat16"),
+    "vs": ("sbuf", [B, KB * B], "bfloat16"),
     "gks": ("sbuf", [B, NG * B], "bfloat16"),
-    "gvs": ("sbuf", [B, NG * VW], "bfloat16"),
+    "gvs": ("sbuf", [B, NG * B], "bfloat16"),
+    "oc": ("sbuf", [B, 8], "bfloat16"),
     "one": ("sbuf", [B, B], "bfloat16"),
     "idn": ("sbuf", [B, B], "bfloat16"),
     "pmx": ("sbuf", [B, 2 * 8], "float32"),
@@ -36,11 +37,12 @@ SCRATCH = {
     "sp3": ("psum", [B, 512], "float32"),
     "sp4": ("psum", [B, 512], "float32"),
     "op": ("psum", [B, 512], "float32"),
+    "lp": ("psum", [B, 512], "float32"),
     "yp": ("psum", [B, 512], "float32"),
 }
-SEMAPHORES = (["qready", "kready", "vready", "gk", "gv", "c0", "c1", "c2", "idr", "lsent",
+SEMAPHORES = (["qready", "kready", "vready", "gk", "gv", "c0", "c1", "c2", "ocr", "idr", "lsent",
                "marr", "mn", "wd", "yd", "rc", "ys", "yst"]
-              + ["%s%d" % (n, p) for n in ("nm", "dgs", "od", "ms") for p in range(2)]
+              + ["%s%d" % (n, p) for n in ("nm", "dgs", "od", "ld", "ms") for p in range(2)]
               + ["%s%d%d" % (n, p, b) for n in ("st", "rd", "sh", "ex") for p in range(2) for b in range(NP)]
               + ["%s%d" % (n, j) for n in ("dj", "oa") for j in range(NS)])
 
@@ -98,10 +100,34 @@ def _q_order(root, sites, topo):
 def _load_kv(g, T):
     S = T.sem
     g.sync.dma_start(T.ks[:], T.k[:, :]).then_inc(S.kready, 16)
-    for b in range(KB):
-        g.sync.dma_start(T.vs[:, VW * b:VW * b + B], T.v[:, B * b:B * b + B]).then_inc(S.vready, 16)
-    for b in range(KB):
-        g.vector.memset(T.vs[:, VW * b + B:VW * (b + 1)], 1.0).then_inc(S.c2, 1)
+    g.scalar.dma_start(T.vs[:], T.v[:, :]).then_inc(S.vready, 16)
+
+
+def _givers(root, sites, far, ship, root_mask):
+    giver = {}
+    for c in far:
+        for x in ship[c]:
+            giver.setdefault(x[0], (c, x[4]))
+    for s in sites:
+        if s != root:
+            giver.setdefault(s, (root, root_mask))
+    return giver
+
+
+def _give_ones(g, core, T, topo, giver):
+    S = T.sem
+    mine = [(d, m) for d, (c, m) in giver.items() if c == core]
+    g.vector.memset(T.oc[:], 1.0).then_inc(S.c2, 1)
+    if not mine:
+        return 0
+    g.wait_ge(S.c2, 1)
+    masks = sorted(set(m for _, m in mine))
+    g.remote_dma_fused(
+        [RemoteDMATransfer(dst_ids=[DstId(rid=topo.addr(d, core)[0], pnc=topo.addr(d, core)[1])
+                                    for d, m in mine if m == mm],
+                           dma_engine_mask=mm, remote_sem=S.ocr, srcs=[T.oc[:]],
+                           dsts=[T.oc[:] for d, m in mine if m == mm], alu_op=0) for mm in masks], local_sem=S.lsent)
+    return sum(_bits(mm) for mm in masks)
 
 
 def _ship(g, core, T, topo, ships):
@@ -116,9 +142,8 @@ def _ship(g, core, T, topo, ships):
 
     g.wait_ge(S.kready, 16)
     call(T.ks, T.gks, B, S.gk)
-    g.wait_ge(S.vready, 16 * KB)
-    g.wait_ge(S.c2, KB)
-    call(T.vs, T.gvs, VW, S.gv)
+    g.wait_ge(S.vready, 16)
+    call(T.vs, T.gvs, B, S.gv)
     return 2 * sum(_bits(x[4]) for x in ships)
 
 
@@ -183,53 +208,63 @@ def _site(g, T, p, blocks, nq, need, negm, msg, after=None):
         act.wait_ge(s2("sh", b), 1)
         act.activation(pt[b], sp[b][:, B:2 * B], ActivationFunctionType.Exp).then_inc(s2("ex", b), 1)
     if after is not None:
-        pe.wait_ge(after, 1)
+        pe.wait_ge(after, 2)
+    pe.wait_ge(need["ones"][0], need["ones"][1])
     for kind, bs in groups:
         for sem, n in need[kind][1]:
             pe.wait_ge(sem, n)
         for b in bs:
             pe.wait_ge(s2("ex", b), 1)
-            mm = pe.matmul(T.op[:, 0:OW], pt[b], blocks[b][1], b == 0, b == nb - 1)
-    mm.then_inc(s1("od"), 1)
+            ml = pe.matmul(T.lp[:, 0:1], pt[b], T.oc[:, 0:1], b == 0, b == nb - 1)
+            if b == nb - 1:
+                ml.then_inc(s1("ld"), 1)
+            mm = pe.matmul(T.op[:, 0:B], pt[b], blocks[b][1], b == 0, b == nb - 1)
+            if b == nb - 1:
+                mm.then_inc(s1("od"), 1)
+    dve.wait_ge(s1("ld"), 1)
+    dve.tensor_copy(msg[1], T.lp[:, 0:1]).then_inc(s1("ms"), 1)
     dve.wait_ge(s1("od"), 1)
-    dve.tensor_copy(msg, T.op[:, 0:OW]).then_inc(s1("ms"), 1)
+    dve.tensor_copy(msg[0], T.op[:, 0:B]).then_inc(s1("ms"), 1)
 
 
 def rank_program(g, core, T, topo):
     cores, root, sites, far, ship, keep, guests = _plan(T, topo)
     S = T.sem
-    if core in far:
-        _load_kv(g, T)
-        g.wait_ge(S.lsent, _ship(g, core, T, topo, ship[core]))
+    if core not in cores:
         return
-    if core not in sites:
-        return
-    slot = sites.index(core)
     away, near = _q_order(root, sites, topo)
     away_mask = topo.mask(root, away[0])
     for c in away:
         away_mask &= topo.mask(root, c)
     near_mask = {c: (topo.mask(root, c) & ~away_mask) for c in near}
+    giver = _givers(root, sites, far, ship, away_mask)
+    if core in far:
+        _load_kv(g, T)
+        left = _give_ones(g, core, T, topo, giver)
+        g.wait_ge(S.lsent, left + _ship(g, core, T, topo, ship[core]))
+        return
+    slot = sites.index(core)
 
     landing = sum(_bits(x[4]) for c in cores for x in ship[c] if x[0] == core)
-    need = {"own": ([(S.kready, 16)], [(S.vready, 16 * KB), (S.c2, KB)]),
-            "guest": ([(S.gk, landing)], [(S.gv, landing)])}
-    own = [(T.ks[:, B * b:B * (b + 1)], T.vs[:, VW * b:VW * b + OW], "own") for b in keep[core]]
-    guest = [(T.gks[:, B * s:B * (s + 1)], T.gvs[:, VW * s:VW * s + OW], "guest") for s in range(guests[core])]
+    need = {"own": ([(S.kready, 16)], [(S.vready, 16)]),
+            "guest": ([(S.gk, landing)], [(S.gv, landing)]),
+            "ones": (S.c2, 1) if core == root else (S.ocr, _bits(giver[core][1]))}
+    own = [(T.ks[:, B * b:B * (b + 1)], T.vs[:, B * b:B * (b + 1)], "own") for b in keep[core]]
+    guest = [(T.gks[:, B * s:B * (s + 1)], T.gvs[:, B * s:B * (s + 1)], "guest") for s in range(guests[core])]
 
     if core != root:
+        _load_kv(g, T)
         _ones(g, T)
         _identity(g, T)
-        _load_kv(g, T)
         left = _ship(g, core, T, topo, ship[core])
         nq = _bits(near_mask[core]) if core in near else _bits(away_mask)
-        _site(g, T, 0, own + guest, nq, need, T.ngm[:, 0:1], T.msg[:, 0:OW])
+        _site(g, T, 0, own + guest, nq, need, T.ngm[:, 0:1], (T.msg[:, 0:B], T.msg[:, B:OW]))
         rid, pid = topo.addr(root, core)
         mask = topo.mask(core, root)
         g.wait_ge(S.nm0, 1)
         g.remote_dma(out_ap=T.mall[:, MW * slot:MW * slot + 1], in_ap=T.ngm[:, 0:1], remote_sem=S.marr,
                      local_sem=S.lsent, pid=pid, routing_id=rid, dma_engine_mask=mask)
-        g.wait_ge(S.ms0, 1)
+        g.wait_ge(S.ms0, 2)
         g.remote_dma(out_ap=T.oland[:, VW * slot:VW * slot + OW], in_ap=T.msg[:, 0:OW], remote_sem=S["oa%d" % slot],
                      local_sem=S.lsent, pid=pid, routing_id=rid, dma_engine_mask=mask)
         g.wait_ge(S.lsent, left + 2 * _bits(mask))
@@ -237,14 +272,15 @@ def rank_program(g, core, T, topo):
 
     pe, dve, act = g.tensor, g.vector, g.scalar
     g.sync.dma_start(T.qs[:], T.q[:, :]).then_inc(S.qready, 16)
-    _ones(g, T)
+    left = _give_ones(g, core, T, topo, giver)
     _load_kv(g, T)
+    _ones(g, T)
     g.wait_ge(S.qready, 16)
     ids = [topo.addr(c, root) for c in away]
     g.remote_dma_fused([RemoteDMATransfer(dst_ids=[DstId(rid=a, pnc=p) for a, p in ids], dma_engine_mask=away_mask,
                                           remote_sem=S.qready, srcs=[T.qs[:]], dsts=[T.qs[:] for _ in ids], alu_op=0)],
                        local_sem=S.lsent)
-    left = _bits(away_mask)
+    left += _bits(away_mask)
     for c in near:
         rid, pid = topo.addr(c, root)
         g.remote_dma(out_ap=T.qs[:], in_ap=T.qs[:], remote_sem=S.qready, local_sem=S.lsent,
@@ -255,9 +291,10 @@ def rank_program(g, core, T, topo):
 
     gslot = len(sites)
     ns = gslot + 1
-    _site(g, T, 0, own, 16, need, T.mall[:, MW * slot:MW * slot + 1], T.oland[:, VW * slot:VW * slot + OW])
-    _site(g, T, 1, guest, 16, need, T.mall[:, MW * gslot:MW * gslot + 1], T.oland[:, VW * gslot:VW * gslot + OW],
-          after=S.ms0)
+    _site(g, T, 0, own, 16, need, T.mall[:, MW * slot:MW * slot + 1],
+          (T.oland[:, VW * slot:VW * slot + B], T.oland[:, VW * slot + B:VW * slot + OW]))
+    _site(g, T, 1, guest, 16, need, T.mall[:, MW * gslot:MW * gslot + 1],
+          (T.oland[:, VW * gslot:VW * gslot + B], T.oland[:, VW * gslot + B:VW * gslot + OW]), after=S.ms0)
 
     n_m = sum(_bits(topo.mask(c, root)) for c in sites if c != root)
     shifts = T.mall[:, 0:ns * MW:MW]
@@ -276,9 +313,9 @@ def rank_program(g, core, T, topo):
     for i, j in enumerate(order):
         pe.wait_ge(S["dj%d" % j], 1)
         if j == slot:
-            pe.wait_ge(S.ms0, 1)
+            pe.wait_ge(S.ms0, 2)
         elif j == gslot:
-            pe.wait_ge(S.ms1, 1)
+            pe.wait_ge(S.ms1, 2)
         else:
             pe.wait_ge(S["oa%d" % j], _bits(topo.mask(sites[j], root)))
         mm = pe.matmul(T.yp[:, 0:OW], T.dg[:, B * j:B * (j + 1)], T.oland[:, VW * j:VW * j + OW],

@@ -2,18 +2,20 @@ from concourse.bass import DstId, RemoteDMATransfer
 from concourse.mybir import AluOpType, AxisListType, ActivationFunctionType
 
 B = 128
+H = B // 2
 KB = 4
 NS = 8
 NG = 5
 NP = 5
-VW = 136
-OW = B + 1
+HB = 72
+VW = HB + H
 MW = 8
 
 SCRATCH = {
     "qs": ("sbuf", [B, B], "bfloat16"),
     "ks": ("sbuf", [B, KB * B], "bfloat16"),
     "vs": ("sbuf", [B, KB * B], "bfloat16"),
+    "vr": ("sbuf", [B, KB * B], "bfloat16"),
     "gks": ("sbuf", [B, NG * B], "bfloat16"),
     "gvs": ("sbuf", [B, NG * B], "bfloat16"),
     "oc": ("sbuf", [B, 8], "bfloat16"),
@@ -40,11 +42,11 @@ SCRATCH = {
     "lp": ("psum", [B, 512], "float32"),
     "yp": ("psum", [B, 512], "float32"),
 }
-SEMAPHORES = (["qready", "kready", "vready", "gk", "gv", "c0", "c1", "c2", "ocr", "idr", "lsent",
-               "marr", "mn", "wd", "yd", "rc", "ys", "yst"]
-              + ["%s%d" % (n, p) for n in ("nm", "dgs", "od", "ld", "ms") for p in range(2)]
+SEMAPHORES = (["qready", "kready", "vready", "gk", "gv", "gw", "vr0", "vr1", "c0", "c1", "c2", "ocr", "idr", "lsent",
+               "marr", "mn", "wd", "yd", "ye", "rc", "ys", "yst"]
+              + ["%s%d" % (n, p) for n in ("nm", "dgs", "od", "oe", "ld", "ms", "mt") for p in range(2)]
               + ["%s%d%d" % (n, p, b) for n in ("st", "rd", "sh", "ex") for p in range(2) for b in range(NP)]
-              + ["%s%d" % (n, j) for n in ("dj", "oa") for j in range(NS)])
+              + ["%s%d" % (n, j) for n in ("dj", "oa", "ob") for j in range(NS)])
 
 
 def _bits(mask):
@@ -79,22 +81,20 @@ def _plan(T, topo):
         for i, s in enumerate(cand):
             ship[c].append((s, per * i, per, guests[s], parts[i]))
             guests[s] += per
+    home = [c for c in sites if _same_chip(topo, c, root)]
     for s in sites:
         if s != root:
-            ship[s].append((root, keep[s].pop(), 1, guests[root], topo.mask(s, root)))
-            guests[root] += 1
+            d = root if s in home else ([c for c in home if topo.die(c) == topo.die(s)] + [root])[0]
+            ship[s].append((d, keep[s].pop(), 1, guests[d], topo.mask(s, d)))
+            guests[d] += 1
     return cores, root, sites, far, ship, keep, guests
 
 
-def _q_order(root, sites, topo):
+def _q_groups(root, sites, topo):
     near = [c for c in sites if c != root and _same_chip(topo, c, root)]
     away = [c for c in sites if c != root and c not in near]
     hosts = sorted(set(topo.host(c) for c in away), reverse=True)
-    rows = [[c for c in away if topo.host(c) == h] for h in hosts]
-    order = []
-    for i in range(max(len(x) for x in rows)):
-        order += [x[i] for x in rows if i < len(x)]
-    return order, near
+    return [[c for c in away if topo.host(c) == h] for h in hosts], near
 
 
 def _load_kv(g, T):
@@ -130,21 +130,41 @@ def _give_ones(g, core, T, topo, giver):
     return sum(_bits(mm) for mm in masks)
 
 
+def _send(g, core, T, topo, items, sem):
+    g.remote_dma_fused(
+        [RemoteDMATransfer(dst_ids=[DstId(rid=topo.addr(d, core)[0], pnc=topo.addr(d, core)[1])],
+                           dma_engine_mask=m, remote_sem=sem, srcs=[src], dsts=[dst], alu_op=0)
+         for d, src, dst, m in items], local_sem=T.sem.lsent)
+
+
 def _ship(g, core, T, topo, ships):
     S = T.sem
-
-    def call(src, dst, w, sem):
-        g.remote_dma_fused(
-            [RemoteDMATransfer(dst_ids=[DstId(rid=topo.addr(d, core)[0], pnc=topo.addr(d, core)[1])],
-                               dma_engine_mask=m, remote_sem=sem, srcs=[src[:, w * b0:w * (b0 + nb)]],
-                               dsts=[dst[:, w * s0:w * (s0 + nb)]], alu_op=0)
-             for d, b0, nb, s0, m in ships], local_sem=S.lsent)
-
     g.wait_ge(S.kready, 16)
-    call(T.ks, T.gks, B, S.gk)
+    _send(g, core, T, topo, [(d, T.ks[:, B * b0:B * (b0 + nb)], T.gks[:, B * s0:B * (s0 + nb)], m)
+                             for d, b0, nb, s0, m in ships], S.gk)
     g.wait_ge(S.vready, 16)
-    call(T.vs, T.gvs, B, S.gv)
+    _send(g, core, T, topo, [(d, T.vs[:, B * b0:B * (b0 + nb)], T.gvs[:, B * s0:B * (s0 + nb)], m)
+                             for d, b0, nb, s0, m in ships], S.gv)
     return 2 * sum(_bits(x[4]) for x in ships)
+
+
+def _ship_far(g, core, T, topo, ships):
+    S = T.sem
+    dve = g.vector
+    dve.wait_ge(S.vready, 16)
+    for h in range(2):
+        for b in range(KB):
+            dve.tensor_copy(T.vr[:, KB * H * h + H * b:KB * H * h + H * (b + 1)],
+                            T.vs[:, B * b + H * h:B * b + H * (h + 1)]).then_inc(S["vr%d" % h], 1)
+    g.wait_ge(S.kready, 16)
+    _send(g, core, T, topo, [(d, T.ks[:, B * b0:B * (b0 + nb)], T.gks[:, B * s0:B * (s0 + nb)], m)
+                             for d, b0, nb, s0, m in ships], S.gk)
+    for h, sem in enumerate((S.gv, S.gw)):
+        g.wait_ge(S["vr%d" % h], KB)
+        _send(g, core, T, topo, [(d, T.vr[:, KB * H * h + H * b0:KB * H * h + H * (b0 + nb)],
+                                  T.gvs[:, NG * H * h + H * s0:NG * H * h + H * (s0 + nb)], m)
+                                 for d, b0, nb, s0, m in ships], sem)
+    return 3 * sum(_bits(x[4]) for x in ships)
 
 
 def _ones(g, T):
@@ -160,7 +180,7 @@ def _identity(g, T):
     g.affine_select(T.idn[:], T.one[:], [[-1, B]], AluOpType.is_equal, 0.0, 0, 1).then_inc(S.idr, 1)
 
 
-def _site(g, T, p, blocks, nq, need, negm, msg, after=None):
+def _site(g, T, p, blocks, nq, need, negm, msg, split, after=()):
     S = T.sem
     pe, dve, act = g.tensor, g.vector, g.scalar
     nb = len(blocks)
@@ -207,24 +227,52 @@ def _site(g, T, p, blocks, nq, need, negm, msg, after=None):
     for b in range(nb):
         act.wait_ge(s2("sh", b), 1)
         act.activation(pt[b], sp[b][:, B:2 * B], ActivationFunctionType.Exp).then_inc(s2("ex", b), 1)
-    if after is not None:
-        pe.wait_ge(after, 2)
+
+    outs = [T.op[:, 0:H], T.yp[:, 0:H]] if split else [T.op[:, 0:B]]
+    fin = {"l": s1("ld"), 0: s1("od"), 1: s1("oe")}
+    ops = []
+    if split:
+        for kind, bs in groups:
+            if kind == "guest":
+                ops += [("l", b, kind) for b in bs] + [(0, b, kind) for b in bs]
+            else:
+                for b in bs:
+                    ops += [("l", b, kind), (0, b, kind)]
+        for kind, bs in groups:
+            ops += [(1, b, kind) for b in bs]
+    else:
+        for kind, bs in groups:
+            for b in bs:
+                ops += [("l", b, kind), (0, b, kind)]
+    first, last = {}, {}
+    for n, op in enumerate(ops):
+        first.setdefault(op[0], n)
+        last[op[0]] = n
+    for sem, n in after:
+        pe.wait_ge(sem, n)
     pe.wait_ge(need["ones"][0], need["ones"][1])
-    for kind, bs in groups:
-        for sem, n in need[kind][1]:
-            pe.wait_ge(sem, n)
-        for b in bs:
+    waited = set()
+    for n, (w, b, kind) in enumerate(ops):
+        if w == "l":
             pe.wait_ge(s2("ex", b), 1)
-            ml = pe.matmul(T.lp[:, 0:1], pt[b], T.oc[:, 0:1], b == 0, b == nb - 1)
-            if b == nb - 1:
-                ml.then_inc(s1("ld"), 1)
-            mm = pe.matmul(T.op[:, 0:B], pt[b], blocks[b][1], b == 0, b == nb - 1)
-            if b == nb - 1:
-                mm.then_inc(s1("od"), 1)
+            mm = pe.matmul(T.lp[:, 0:1], pt[b], T.oc[:, 0:1], first[w] == n, last[w] == n)
+        else:
+            if (kind, w) not in waited:
+                waited.add((kind, w))
+                for sem, cnt in need[kind][1][w]:
+                    pe.wait_ge(sem, cnt)
+            mm = pe.matmul(outs[w], pt[b], blocks[b][1][w], first[w] == n, last[w] == n)
+        if last[w] == n:
+            mm.then_inc(fin[w], 1)
     dve.wait_ge(s1("ld"), 1)
-    dve.tensor_copy(msg[1], T.lp[:, 0:1]).then_inc(s1("ms"), 1)
+    dve.tensor_copy(msg[2], T.lp[:, 0:1]).then_inc(s1("ms"), 1)
     dve.wait_ge(s1("od"), 1)
-    dve.tensor_copy(msg[0], T.op[:, 0:B]).then_inc(s1("ms"), 1)
+    dve.tensor_copy(msg[0], T.op[:, 0:H]).then_inc(s1("ms"), 1)
+    if split:
+        dve.wait_ge(s1("oe"), 1)
+        dve.tensor_copy(msg[1], T.yp[:, 0:H]).then_inc(s1("mt"), 1)
+    else:
+        dve.tensor_copy(msg[1], T.op[:, H:B]).then_inc(s1("mt"), 1)
 
 
 def rank_program(g, core, T, topo):
@@ -232,55 +280,71 @@ def rank_program(g, core, T, topo):
     S = T.sem
     if core not in cores:
         return
-    away, near = _q_order(root, sites, topo)
+    rows, near = _q_groups(root, sites, topo)
+    away = [c for x in rows for c in x]
     away_mask = topo.mask(root, away[0])
     for c in away:
         away_mask &= topo.mask(root, c)
+    q_parts = _split(away_mask, len(rows))
+    q_mask = {c: q_parts[i] for i, x in enumerate(rows) for c in x}
     near_mask = {c: (topo.mask(root, c) & ~away_mask) for c in near}
     giver = _givers(root, sites, far, ship, away_mask)
     if core in far:
         _load_kv(g, T)
         left = _give_ones(g, core, T, topo, giver)
-        g.wait_ge(S.lsent, left + _ship(g, core, T, topo, ship[core]))
+        g.wait_ge(S.lsent, left + _ship_far(g, core, T, topo, ship[core]))
         return
     slot = sites.index(core)
-
     landing = sum(_bits(x[4]) for c in cores for x in ship[c] if x[0] == core)
-    need = {"own": ([(S.kready, 16)], [(S.vready, 16)]),
-            "guest": ([(S.gk, landing)], [(S.gv, landing)]),
-            "ones": (S.c2, 1) if core == root else (S.ocr, _bits(giver[core][1]))}
-    own = [(T.ks[:, B * b:B * (b + 1)], T.vs[:, B * b:B * (b + 1)], "own") for b in keep[core]]
-    guest = [(T.gks[:, B * s:B * (s + 1)], T.gvs[:, B * s:B * (s + 1)], "guest") for s in range(guests[core])]
 
     if core != root:
+        halves = any(x[0] == core for c in far for x in ship[c])
+        need = {"own": ([(S.kready, 16)], [[(S.vready, 16)], [(S.vready, 16)]]),
+                "guest": ([(S.gk, landing)], [[(S.gv, landing)], [(S.gw if halves else S.gv, landing)]]),
+                "ones": (S.ocr, _bits(giver[core][1]))}
+        own = [(T.ks[:, B * b:B * (b + 1)], [T.vs[:, B * b:B * b + H], T.vs[:, B * b + H:B * (b + 1)]], "own")
+               for b in keep[core]]
+        guest = [(T.gks[:, B * s:B * (s + 1)],
+                  [T.gvs[:, H * s:H * (s + 1)], T.gvs[:, NG * H + H * s:NG * H + H * (s + 1)]] if halves else
+                  [T.gvs[:, B * s:B * s + H], T.gvs[:, B * s + H:B * (s + 1)]], "guest")
+                 for s in range(guests[core])]
         _load_kv(g, T)
         _ones(g, T)
         _identity(g, T)
         left = _ship(g, core, T, topo, ship[core])
-        nq = _bits(near_mask[core]) if core in near else _bits(away_mask)
-        _site(g, T, 0, own + guest, nq, need, T.ngm[:, 0:1], (T.msg[:, 0:B], T.msg[:, B:OW]))
+        nq = _bits(near_mask[core]) if core in near else _bits(q_mask[core])
+        _site(g, T, 0, own + guest, nq, need, T.ngm[:, 0:1],
+              (T.msg[:, 0:H], T.msg[:, HB:HB + H], T.msg[:, H:H + 1]), True)
         rid, pid = topo.addr(root, core)
         mask = topo.mask(core, root)
         g.wait_ge(S.nm0, 1)
         g.remote_dma(out_ap=T.mall[:, MW * slot:MW * slot + 1], in_ap=T.ngm[:, 0:1], remote_sem=S.marr,
                      local_sem=S.lsent, pid=pid, routing_id=rid, dma_engine_mask=mask)
         g.wait_ge(S.ms0, 2)
-        g.remote_dma(out_ap=T.oland[:, VW * slot:VW * slot + OW], in_ap=T.msg[:, 0:OW], remote_sem=S["oa%d" % slot],
-                     local_sem=S.lsent, pid=pid, routing_id=rid, dma_engine_mask=mask)
-        g.wait_ge(S.lsent, left + 2 * _bits(mask))
+        g.remote_dma(out_ap=T.oland[:, VW * slot:VW * slot + H + 1], in_ap=T.msg[:, 0:H + 1],
+                     remote_sem=S["oa%d" % slot], local_sem=S.lsent, pid=pid, routing_id=rid, dma_engine_mask=mask)
+        g.wait_ge(S.mt0, 1)
+        g.remote_dma(out_ap=T.oland[:, VW * slot + HB:VW * slot + HB + H], in_ap=T.msg[:, HB:HB + H],
+                     remote_sem=S["ob%d" % slot], local_sem=S.lsent, pid=pid, routing_id=rid, dma_engine_mask=mask)
+        g.wait_ge(S.lsent, left + 3 * _bits(mask))
         return
 
     pe, dve, act = g.tensor, g.vector, g.scalar
+    need = {"own": ([(S.kready, 16)], [[(S.vready, 16)]]),
+            "guest": ([(S.gk, landing)], [[(S.gv, landing)]]),
+            "ones": (S.c2, 1)}
+    own = [(T.ks[:, B * b:B * (b + 1)], [T.vs[:, B * b:B * (b + 1)]], "own") for b in keep[core]]
+    guest = [(T.gks[:, B * s:B * (s + 1)], [T.gvs[:, B * s:B * (s + 1)]], "guest") for s in range(guests[core])]
     g.sync.dma_start(T.qs[:], T.q[:, :]).then_inc(S.qready, 16)
     left = _give_ones(g, core, T, topo, giver)
     _load_kv(g, T)
     _ones(g, T)
     g.wait_ge(S.qready, 16)
-    ids = [topo.addr(c, root) for c in away]
-    g.remote_dma_fused([RemoteDMATransfer(dst_ids=[DstId(rid=a, pnc=p) for a, p in ids], dma_engine_mask=away_mask,
-                                          remote_sem=S.qready, srcs=[T.qs[:]], dsts=[T.qs[:] for _ in ids], alu_op=0)],
-                       local_sem=S.lsent)
-    left += _bits(away_mask)
+    g.remote_dma_fused(
+        [RemoteDMATransfer(dst_ids=[DstId(rid=topo.addr(c, root)[0], pnc=topo.addr(c, root)[1]) for c in x],
+                           dma_engine_mask=q_parts[i], remote_sem=S.qready, srcs=[T.qs[:]],
+                           dsts=[T.qs[:] for _ in x], alu_op=0) for i, x in enumerate(rows)], local_sem=S.lsent)
+    left += sum(_bits(m) for m in q_parts)
     for c in near:
         rid, pid = topo.addr(c, root)
         g.remote_dma(out_ap=T.qs[:], in_ap=T.qs[:], remote_sem=S.qready, local_sem=S.lsent,
@@ -291,10 +355,14 @@ def rank_program(g, core, T, topo):
 
     gslot = len(sites)
     ns = gslot + 1
-    _site(g, T, 0, own, 16, need, T.mall[:, MW * slot:MW * slot + 1],
-          (T.oland[:, VW * slot:VW * slot + B], T.oland[:, VW * slot + B:VW * slot + OW]))
-    _site(g, T, 1, guest, 16, need, T.mall[:, MW * gslot:MW * gslot + 1],
-          (T.oland[:, VW * gslot:VW * gslot + B], T.oland[:, VW * gslot + B:VW * gslot + OW]), after=S.ms0)
+
+    def place(j):
+        return (T.oland[:, VW * j:VW * j + H], T.oland[:, VW * j + HB:VW * j + HB + H],
+                T.oland[:, VW * j + H:VW * j + H + 1])
+
+    _site(g, T, 0, own, 16, need, T.mall[:, MW * slot:MW * slot + 1], place(slot), False)
+    _site(g, T, 1, guest, 16, need, T.mall[:, MW * gslot:MW * gslot + 1], place(gslot), False,
+          after=[(S.ms0, 2), (S.mt0, 1)])
 
     n_m = sum(_bits(topo.mask(c, root)) for c in sites if c != root)
     shifts = T.mall[:, 0:ns * MW:MW]
@@ -305,26 +373,36 @@ def rank_program(g, core, T, topo):
     act.wait_ge(S.nm1, 1)
     act.wait_ge(S.mn, 1)
     act.activation(T.wv[:, 0:ns], shifts, ActivationFunctionType.Exp, bias=T.mng[:, 0:1], scale=-1.0).then_inc(S.wd, 1)
-    order = [slot, gslot] + [sites.index(c) for c in near + away]
+    early = [slot, gslot] + [sites.index(c) for c in near]
+    late = [sites.index(c) for c in away]
     dve.wait_ge(S.wd, 1)
-    for j in order:
+    for j in early + late:
         dve.tensor_scalar(T.dg[:, B * j:B * (j + 1)], T.idn[:], T.wv[:, j:j + 1], None,
                           AluOpType.mult).then_inc(S["dj%d" % j], 1)
-    for i, j in enumerate(order):
-        pe.wait_ge(S["dj%d" % j], 1)
+    seq = [(h, j) for j in early for h in range(2)] + [(h, j) for h in range(2) for j in late]
+    for h, j in seq:
+        if h == 0:
+            pe.wait_ge(S["dj%d" % j], 1)
         if j == slot:
-            pe.wait_ge(S.ms0, 2)
+            pe.wait_ge(S.mt0 if h else S.ms0, 1 if h else 2)
         elif j == gslot:
-            pe.wait_ge(S.ms1, 2)
+            pe.wait_ge(S.mt1 if h else S.ms1, 1 if h else 2)
         else:
-            pe.wait_ge(S["oa%d" % j], _bits(topo.mask(sites[j], root)))
-        mm = pe.matmul(T.yp[:, 0:OW], T.dg[:, B * j:B * (j + 1)], T.oland[:, VW * j:VW * j + OW],
-                       i == 0, i == len(order) - 1)
-    mm.then_inc(S.yd, 1)
+            pe.wait_ge(S["%s%d" % ("ob" if h else "oa", j)], _bits(topo.mask(sites[j], root)))
+        if h == 0:
+            mm = pe.matmul(T.yp[:, 0:H + 1], T.dg[:, B * j:B * (j + 1)], T.oland[:, VW * j:VW * j + H + 1],
+                           j == seq[0][1], j == late[-1])
+        else:
+            mm = pe.matmul(T.sp0[:, 0:H], T.dg[:, B * j:B * (j + 1)], T.oland[:, VW * j + HB:VW * j + HB + H],
+                           j == seq[0][1], j == late[-1])
+        if j == late[-1]:
+            mm.then_inc(S.ye if h else S.yd, 1)
     dve.wait_ge(S.yd, 1)
-    dve.reciprocal(T.rcp[:, 0:1], T.yp[:, B:OW]).then_inc(S.rc, 1)
+    dve.reciprocal(T.rcp[:, 0:1], T.yp[:, H:H + 1]).then_inc(S.rc, 1)
     dve.wait_ge(S.rc, 1)
-    dve.tensor_scalar(T.ysb[:], T.yp[:, 0:B], T.rcp[:, 0:1], None, AluOpType.mult).then_inc(S.ys, 1)
-    g.sync.wait_ge(S.ys, 1)
+    dve.tensor_scalar(T.ysb[:, 0:H], T.yp[:, 0:H], T.rcp[:, 0:1], None, AluOpType.mult).then_inc(S.ys, 1)
+    dve.wait_ge(S.ye, 1)
+    dve.tensor_scalar(T.ysb[:, H:B], T.sp0[:, 0:H], T.rcp[:, 0:1], None, AluOpType.mult).then_inc(S.ys, 1)
+    g.sync.wait_ge(S.ys, 2)
     g.sync.dma_start(T.y[:, :], T.ysb[:]).then_inc(S.yst, 16)
     g.sync.wait_ge(S.yst, 16)

from concourse.bass import DstId, RemoteDMATransfer
from concourse.mybir import AluOpType, AxisListType, ActivationFunctionType

B = 128
H = B // 2
KB = 4
NS = 8
NG = 5
NP = 5
HB = 72
VW = HB + H
MW = 8

SCRATCH = {
    "qs": ("sbuf", [B, B], "bfloat16"),
    "ks": ("sbuf", [B, KB * B], "bfloat16"),
    "vs": ("sbuf", [B, KB * B], "bfloat16"),
    "vr": ("sbuf", [B, KB * B], "bfloat16"),
    "gks": ("sbuf", [B, NG * B], "bfloat16"),
    "gvs": ("sbuf", [B, NG * B], "bfloat16"),
    "oc": ("sbuf", [B, 8], "bfloat16"),
    "one": ("sbuf", [B, B], "bfloat16"),
    "idn": ("sbuf", [B, B], "bfloat16"),
    "pmx": ("sbuf", [B, 2 * 8], "float32"),
    "ngm": ("sbuf", [B, MW], "bfloat16"),
    "dgm": ("sbuf", [B, 2 * B], "bfloat16"),
    "pt": ("sbuf", [B, 2 * NP * B], "bfloat16"),
    "msg": ("sbuf", [B, VW], "bfloat16"),
    "mall": ("sbuf", [B, NS * MW], "bfloat16"),
    "oland": ("sbuf", [B, NS * VW], "bfloat16"),
    "mng": ("sbuf", [B, 1], "float32"),
    "wv": ("sbuf", [B, NS], "float32"),
    "dg": ("sbuf", [B, NS * B], "bfloat16"),
    "rcp": ("sbuf", [B, 1], "float32"),
    "ysb": ("sbuf", [B, B], "bfloat16"),
    "sp0": ("psum", [B, 512], "float32"),
    "sp1": ("psum", [B, 512], "float32"),
    "sp2": ("psum", [B, 512], "float32"),
    "sp3": ("psum", [B, 512], "float32"),
    "sp4": ("psum", [B, 512], "float32"),
    "op": ("psum", [B, 512], "float32"),
    "lp": ("psum", [B, 512], "float32"),
    "yp": ("psum", [B, 512], "float32"),
}
SEMAPHORES = (["qready", "kready", "vready", "gk", "gv", "gw", "vr0", "vr1", "c0", "c1", "c2", "ocr", "idr", "lsent",
               "marr", "mn", "wd", "yd", "ye", "rc", "ys", "yst"]
              + ["%s%d" % (n, p) for n in ("nm", "dgs", "od", "oe", "ld", "ms", "mt") for p in range(2)]
              + ["%s%d%d" % (n, p, b) for n in ("st", "rd", "sh", "ex") for p in range(2) for b in range(NP)]
              + ["%s%d" % (n, j) for n in ("dj", "oa", "ob") for j in range(NS)])


def _bits(mask):
    return bin(mask).count("1")


def _split(mask, n):
    eng = [i for i in range(mask.bit_length()) if (mask >> i) & 1]
    per = len(eng) // n
    return [sum(1 << i for i in eng[j * per:(j + 1) * per]) for j in range(n)]


def _same_chip(topo, a, b):
    return topo.host(a) == topo.host(b) and topo.chip(a) == topo.chip(b)


def _plan(T, topo):
    cores = [int(c) for c in T.cores]
    root = cores[T.root]
    sites = [c for c in cores if c == root or (topo.may_write(root, c) and topo.may_write(c, root))]
    far = [c for c in cores if c not in sites]
    ship = {c: [] for c in cores}
    keep = {c: list(range(KB)) for c in sites}
    guests = {c: 0 for c in sites}
    for c in far:
        cand = [s for s in sites if topo.may_write(c, s) and topo.die(s) == topo.die(c)]
        common = topo.mask(c, cand[0])
        for s in cand:
            common &= topo.mask(c, s)
        parts = _split(common, len(cand))
        per = KB // len(cand)
        for i, s in enumerate(cand):
            ship[c].append((s, per * i, per, guests[s], parts[i]))
            guests[s] += per
    home = [c for c in sites if _same_chip(topo, c, root)]
    for s in sites:
        if s != root:
            d = root if s in home else ([c for c in home if topo.die(c) == topo.die(s)] + [root])[0]
            ship[s].append((d, keep[s].pop(), 1, guests[d], topo.mask(s, d)))
            guests[d] += 1
    return cores, root, sites, far, ship, keep, guests


def _q_groups(root, sites, topo):
    near = [c for c in sites if c != root and _same_chip(topo, c, root)]
    away = [c for c in sites if c != root and c not in near]
    hosts = sorted(set(topo.host(c) for c in away), reverse=True)
    return [[c for c in away if topo.host(c) == h] for h in hosts], near


def _load_kv(g, T):
    S = T.sem
    g.sync.dma_start(T.ks[:], T.k[:, :]).then_inc(S.kready, 16)
    g.scalar.dma_start(T.vs[:], T.v[:, :]).then_inc(S.vready, 16)


def _givers(root, sites, far, ship, root_mask):
    giver = {}
    for c in far:
        for x in ship[c]:
            giver.setdefault(x[0], (c, x[4]))
    for s in sites:
        if s != root:
            giver.setdefault(s, (root, root_mask))
    return giver


def _give_ones(g, core, T, topo, giver):
    S = T.sem
    mine = [(d, m) for d, (c, m) in giver.items() if c == core]
    g.vector.memset(T.oc[:], 1.0).then_inc(S.c2, 1)
    if not mine:
        return 0
    g.wait_ge(S.c2, 1)
    masks = sorted(set(m for _, m in mine))
    g.remote_dma_fused(
        [RemoteDMATransfer(dst_ids=[DstId(rid=topo.addr(d, core)[0], pnc=topo.addr(d, core)[1])
                                    for d, m in mine if m == mm],
                           dma_engine_mask=mm, remote_sem=S.ocr, srcs=[T.oc[:]],
                           dsts=[T.oc[:] for d, m in mine if m == mm], alu_op=0) for mm in masks], local_sem=S.lsent)
    return sum(_bits(mm) for mm in masks)


def _send(g, core, T, topo, items, sem):
    g.remote_dma_fused(
        [RemoteDMATransfer(dst_ids=[DstId(rid=topo.addr(d, core)[0], pnc=topo.addr(d, core)[1])],
                           dma_engine_mask=m, remote_sem=sem, srcs=[src], dsts=[dst], alu_op=0)
         for d, src, dst, m in items], local_sem=T.sem.lsent)


def _ship(g, core, T, topo, ships):
    S = T.sem
    g.wait_ge(S.kready, 16)
    _send(g, core, T, topo, [(d, T.ks[:, B * b0:B * (b0 + nb)], T.gks[:, B * s0:B * (s0 + nb)], m)
                             for d, b0, nb, s0, m in ships], S.gk)
    g.wait_ge(S.vready, 16)
    _send(g, core, T, topo, [(d, T.vs[:, B * b0:B * (b0 + nb)], T.gvs[:, B * s0:B * (s0 + nb)], m)
                             for d, b0, nb, s0, m in ships], S.gv)
    return 2 * sum(_bits(x[4]) for x in ships)


def _ship_far(g, core, T, topo, ships):
    S = T.sem
    dve = g.vector
    dve.wait_ge(S.vready, 16)
    for h in range(2):
        for b in range(KB):
            dve.tensor_copy(T.vr[:, KB * H * h + H * b:KB * H * h + H * (b + 1)],
                            T.vs[:, B * b + H * h:B * b + H * (h + 1)]).then_inc(S["vr%d" % h], 1)
    g.wait_ge(S.kready, 16)
    _send(g, core, T, topo, [(d, T.ks[:, B * b0:B * (b0 + nb)], T.gks[:, B * s0:B * (s0 + nb)], m)
                             for d, b0, nb, s0, m in ships], S.gk)
    for h, sem in enumerate((S.gv, S.gw)):
        g.wait_ge(S["vr%d" % h], KB)
        _send(g, core, T, topo, [(d, T.vr[:, KB * H * h + H * b0:KB * H * h + H * (b0 + nb)],
                                  T.gvs[:, NG * H * h + H * s0:NG * H * h + H * (s0 + nb)], m)
                                 for d, b0, nb, s0, m in ships], sem)
    return 3 * sum(_bits(x[4]) for x in ships)


def _ones(g, T):
    S = T.sem
    g.vector.memset(T.one[:], 0.0).then_inc(S.c0, 1)
    g.scalar.wait_ge(S.c0, 1)
    g.scalar.activation(T.one[:], T.one[:], ActivationFunctionType.Exp).then_inc(S.c1, 1)


def _identity(g, T):
    S = T.sem
    g.wait_ge(S.c1, 1)
    g.affine_select(T.idn[:], T.one[:], [[-1, B]], AluOpType.is_equal, 0.0, 0, 1).then_inc(S.idr, 1)


def _site(g, T, p, blocks, nq, need, negm, msg, split, after=()):
    S = T.sem
    pe, dve, act = g.tensor, g.vector, g.scalar
    nb = len(blocks)
    sp = [T["sp%d" % b] for b in range(nb)]
    pt = [T.pt[:, B * (NP * p + b):B * (NP * p + b + 1)] for b in range(nb)]
    dgm = T.dgm[:, B * p:B * (p + 1)]

    def s1(n):
        return S["%s%d" % (n, p)]

    def s2(n, b):
        return S["%s%d%d" % (n, p, b)]

    groups = []
    for b, blk in enumerate(blocks):
        if not groups or groups[-1][0] != blk[2]:
            groups.append((blk[2], []))
        groups[-1][1].append(b)

    pe.wait_ge(S.qready, nq)
    for kind, bs in groups:
        for sem, n in need[kind][0]:
            pe.wait_ge(sem, n)
        for b in bs:
            pe.matmul(sp[b][:, 0:B], T.qs[:], blocks[b][0], True, True).then_inc(s2("st", b), 1)
        for b in bs:
            pe.wait_ge(s2("rd", b), 1)
            pe.matmul(sp[b][:, B:2 * B], blocks[b][0], T.qs[:], True, False)
    for b in range(nb):
        dve.wait_ge(s2("st", b), 1)
        dve.tensor_reduce(T.pmx[:, 8 * p + b:8 * p + b + 1], sp[b][:, 0:B], AxisListType.X,
                          AluOpType.max).then_inc(s2("rd", b), 1)
    for b in range(nb):
        dve.wait_ge(s2("rd", b), 1)
    dve.tensor_reduce(negm, T.pmx[:, 8 * p:8 * p + nb], AxisListType.X, AluOpType.max, negate=True).then_inc(s1("nm"), 1)
    dve.wait_ge(s1("nm"), 1)
    dve.wait_ge(S.idr, 1)
    dve.tensor_scalar(dgm, T.idn[:], negm, None, AluOpType.mult).then_inc(s1("dgs"), 1)

    pe.wait_ge(S.c1, 1)
    pe.wait_ge(s1("dgs"), 1)
    for b in range(nb):
        pe.matmul(sp[b][:, B:2 * B], T.one[:], dgm, False, True).then_inc(s2("sh", b), 1)
    for b in range(nb):
        act.wait_ge(s2("sh", b), 1)
        act.activation(pt[b], sp[b][:, B:2 * B], ActivationFunctionType.Exp).then_inc(s2("ex", b), 1)

    outs = [T.op[:, 0:H], T.yp[:, 0:H]] if split else [T.op[:, 0:B]]
    fin = {"l": s1("ld"), 0: s1("od"), 1: s1("oe")}
    ops = []
    if split:
        for kind, bs in groups:
            if kind == "guest":
                ops += [("l", b, kind) for b in bs] + [(0, b, kind) for b in bs]
            else:
                for b in bs:
                    ops += [("l", b, kind), (0, b, kind)]
        for kind, bs in groups:
            ops += [(1, b, kind) for b in bs]
    else:
        for kind, bs in groups:
            for b in bs:
                ops += [("l", b, kind), (0, b, kind)]
    first, last = {}, {}
    for n, op in enumerate(ops):
        first.setdefault(op[0], n)
        last[op[0]] = n
    for sem, n in after:
        pe.wait_ge(sem, n)
    pe.wait_ge(need["ones"][0], need["ones"][1])
    waited = set()
    for n, (w, b, kind) in enumerate(ops):
        if w == "l":
            pe.wait_ge(s2("ex", b), 1)
            mm = pe.matmul(T.lp[:, 0:1], pt[b], T.oc[:, 0:1], first[w] == n, last[w] == n)
        else:
            if (kind, w) not in waited:
                waited.add((kind, w))
                for sem, cnt in need[kind][1][w]:
                    pe.wait_ge(sem, cnt)
            mm = pe.matmul(outs[w], pt[b], blocks[b][1][w], first[w] == n, last[w] == n)
        if last[w] == n:
            mm.then_inc(fin[w], 1)
    dve.wait_ge(s1("ld"), 1)
    dve.tensor_copy(msg[2], T.lp[:, 0:1]).then_inc(s1("ms"), 1)
    dve.wait_ge(s1("od"), 1)
    dve.tensor_copy(msg[0], T.op[:, 0:H]).then_inc(s1("ms"), 1)
    if split:
        dve.wait_ge(s1("oe"), 1)
        dve.tensor_copy(msg[1], T.yp[:, 0:H]).then_inc(s1("mt"), 1)
    else:
        dve.tensor_copy(msg[1], T.op[:, H:B]).then_inc(s1("mt"), 1)


def rank_program(g, core, T, topo):
    cores, root, sites, far, ship, keep, guests = _plan(T, topo)
    S = T.sem
    if core not in cores:
        return
    rows, near = _q_groups(root, sites, topo)
    away = [c for x in rows for c in x]
    away_mask = topo.mask(root, away[0])
    for c in away:
        away_mask &= topo.mask(root, c)
    q_parts = _split(away_mask, len(rows))
    q_mask = {c: q_parts[i] for i, x in enumerate(rows) for c in x}
    near_mask = {c: (topo.mask(root, c) & ~away_mask) for c in near}
    giver = _givers(root, sites, far, ship, away_mask)
    if core in far:
        _load_kv(g, T)
        left = _give_ones(g, core, T, topo, giver)
        g.wait_ge(S.lsent, left + _ship_far(g, core, T, topo, ship[core]))
        return
    slot = sites.index(core)
    landing = sum(_bits(x[4]) for c in cores for x in ship[c] if x[0] == core)

    if core != root:
        halves = any(x[0] == core for c in far for x in ship[c])
        need = {"own": ([(S.kready, 16)], [[(S.vready, 16)], [(S.vready, 16)]]),
                "guest": ([(S.gk, landing)], [[(S.gv, landing)], [(S.gw if halves else S.gv, landing)]]),
                "ones": (S.ocr, _bits(giver[core][1]))}
        own = [(T.ks[:, B * b:B * (b + 1)], [T.vs[:, B * b:B * b + H], T.vs[:, B * b + H:B * (b + 1)]], "own")
               for b in keep[core]]
        guest = [(T.gks[:, B * s:B * (s + 1)],
                  [T.gvs[:, H * s:H * (s + 1)], T.gvs[:, NG * H + H * s:NG * H + H * (s + 1)]] if halves else
                  [T.gvs[:, B * s:B * s + H], T.gvs[:, B * s + H:B * (s + 1)]], "guest")
                 for s in range(guests[core])]
        _load_kv(g, T)
        _ones(g, T)
        _identity(g, T)
        left = _ship(g, core, T, topo, ship[core])
        nq = _bits(near_mask[core]) if core in near else _bits(q_mask[core])
        _site(g, T, 0, own + guest, nq, need, T.ngm[:, 0:1],
              (T.msg[:, 0:H], T.msg[:, HB:HB + H], T.msg[:, H:H + 1]), True)
        rid, pid = topo.addr(root, core)
        mask = topo.mask(core, root)
        g.wait_ge(S.nm0, 1)
        g.remote_dma(out_ap=T.mall[:, MW * slot:MW * slot + 1], in_ap=T.ngm[:, 0:1], remote_sem=S.marr,
                     local_sem=S.lsent, pid=pid, routing_id=rid, dma_engine_mask=mask)
        g.wait_ge(S.ms0, 2)
        g.remote_dma(out_ap=T.oland[:, VW * slot:VW * slot + H + 1], in_ap=T.msg[:, 0:H + 1],
                     remote_sem=S["oa%d" % slot], local_sem=S.lsent, pid=pid, routing_id=rid, dma_engine_mask=mask)
        g.wait_ge(S.mt0, 1)
        g.remote_dma(out_ap=T.oland[:, VW * slot + HB:VW * slot + HB + H], in_ap=T.msg[:, HB:HB + H],
                     remote_sem=S["ob%d" % slot], local_sem=S.lsent, pid=pid, routing_id=rid, dma_engine_mask=mask)
        g.wait_ge(S.lsent, left + 3 * _bits(mask))
        return

    pe, dve, act = g.tensor, g.vector, g.scalar
    need = {"own": ([(S.kready, 16)], [[(S.vready, 16)]]),
            "guest": ([(S.gk, landing)], [[(S.gv, landing)]]),
            "ones": (S.c2, 1)}
    own = [(T.ks[:, B * b:B * (b + 1)], [T.vs[:, B * b:B * (b + 1)]], "own") for b in keep[core]]
    guest = [(T.gks[:, B * s:B * (s + 1)], [T.gvs[:, B * s:B * (s + 1)]], "guest") for s in range(guests[core])]
    g.sync.dma_start(T.qs[:], T.q[:, :]).then_inc(S.qready, 16)
    left = _give_ones(g, core, T, topo, giver)
    _load_kv(g, T)
    _ones(g, T)
    g.wait_ge(S.qready, 16)
    g.remote_dma_fused(
        [RemoteDMATransfer(dst_ids=[DstId(rid=topo.addr(c, root)[0], pnc=topo.addr(c, root)[1]) for c in x],
                           dma_engine_mask=q_parts[i], remote_sem=S.qready, srcs=[T.qs[:]],
                           dsts=[T.qs[:] for _ in x], alu_op=0) for i, x in enumerate(rows)], local_sem=S.lsent)
    left += sum(_bits(m) for m in q_parts)
    for c in near:
        rid, pid = topo.addr(c, root)
        g.remote_dma(out_ap=T.qs[:], in_ap=T.qs[:], remote_sem=S.qready, local_sem=S.lsent,
                     pid=pid, routing_id=rid, dma_engine_mask=near_mask[c])
        left += _bits(near_mask[c])
    _identity(g, T)
    g.wait_ge(S.lsent, left)

    gslot = len(sites)
    ns = gslot + 1

    def place(j):
        return (T.oland[:, VW * j:VW * j + H], T.oland[:, VW * j + HB:VW * j + HB + H],
                T.oland[:, VW * j + H:VW * j + H + 1])

    _site(g, T, 0, own, 16, need, T.mall[:, MW * slot:MW * slot + 1], place(slot), False)
    _site(g, T, 1, guest, 16, need, T.mall[:, MW * gslot:MW * gslot + 1], place(gslot), False,
          after=[(S.ms0, 2), (S.mt0, 1)])

    n_m = sum(_bits(topo.mask(c, root)) for c in sites if c != root)
    shifts = T.mall[:, 0:ns * MW:MW]
    dve.wait_ge(S.marr, n_m)
    dve.tensor_reduce(T.mng[:, 0:1], shifts, AxisListType.X, AluOpType.min).then_inc(S.mn, 1)
    act.wait_ge(S.marr, n_m)
    act.wait_ge(S.nm0, 1)
    act.wait_ge(S.nm1, 1)
    act.wait_ge(S.mn, 1)
    act.activation(T.wv[:, 0:ns], shifts, ActivationFunctionType.Exp, bias=T.mng[:, 0:1], scale=-1.0).then_inc(S.wd, 1)
    early = [slot, gslot] + [sites.index(c) for c in near]
    late = [sites.index(c) for c in away]
    dve.wait_ge(S.wd, 1)
    for j in early + late:
        dve.tensor_scalar(T.dg[:, B * j:B * (j + 1)], T.idn[:], T.wv[:, j:j + 1], None,
                          AluOpType.mult).then_inc(S["dj%d" % j], 1)
    seq = [(h, j) for j in early for h in range(2)] + [(h, j) for h in range(2) for j in late]
    for h, j in seq:
        if h == 0:
            pe.wait_ge(S["dj%d" % j], 1)
        if j == slot:
            pe.wait_ge(S.mt0 if h else S.ms0, 1 if h else 2)
        elif j == gslot:
            pe.wait_ge(S.mt1 if h else S.ms1, 1 if h else 2)
        else:
            pe.wait_ge(S["%s%d" % ("ob" if h else "oa", j)], _bits(topo.mask(sites[j], root)))
        if h == 0:
            mm = pe.matmul(T.yp[:, 0:H + 1], T.dg[:, B * j:B * (j + 1)], T.oland[:, VW * j:VW * j + H + 1],
                           j == seq[0][1], j == late[-1])
        else:
            mm = pe.matmul(T.sp0[:, 0:H], T.dg[:, B * j:B * (j + 1)], T.oland[:, VW * j + HB:VW * j + HB + H],
                           j == seq[0][1], j == late[-1])
        if j == late[-1]:
            mm.then_inc(S.ye if h else S.yd, 1)
    dve.wait_ge(S.yd, 1)
    dve.reciprocal(T.rcp[:, 0:1], T.yp[:, H:H + 1]).then_inc(S.rc, 1)
    dve.wait_ge(S.rc, 1)
    dve.tensor_scalar(T.ysb[:, 0:H], T.yp[:, 0:H], T.rcp[:, 0:1], None, AluOpType.mult).then_inc(S.ys, 1)
    dve.wait_ge(S.ye, 1)
    dve.tensor_scalar(T.ysb[:, H:B], T.sp0[:, 0:H], T.rcp[:, 0:1], None, AluOpType.mult).then_inc(S.ys, 1)
    g.sync.wait_ge(S.ys, 2)
    g.sync.dma_start(T.y[:, :], T.ysb[:]).then_inc(S.yst, 16)
    g.sync.wait_ge(S.yst, 16)
